import numpy as np, ml_dtypes
CORES = [3,7,11,15,131,135,139,143]
N = 8
import mx_ref
BF = ml_dtypes.bfloat16
def gentries(a):
    return np.ascontiguousarray(a.reshape(8, 16, -1).transpose(0, 2, 1)).reshape(8, -1)
def gtable(e):
    e = np.asarray(e); return np.ascontiguousarray(e.reshape(8, -1, 16).transpose(0, 2, 1)).reshape(128, -1).astype(np.int32)
def gcols(t, e):
    v = np.concatenate([t.reshape(8, 16, -1, 4), np.zeros((8, 16, 1, 4), BF)], axis=2)
    return np.ascontiguousarray(np.stack([v[g][:, e[g]] for g in range(8)])).reshape(128, -1)
def tile(rs):
    return np.stack(rs, axis=2).reshape(128, -1).astype(BF)
def pick(q, e):
    c = np.concatenate([q[0].reshape(128, -1, 4), np.zeros((128, 1, 4), np.uint8)], axis=1); s = np.concatenate([q[1], np.ones((16, 1), np.uint8)], axis=1)
    return (np.ascontiguousarray(c[:, e].reshape(128, -1)), np.ascontiguousarray(s[:, e]))
def join(*qs):
    return (np.concatenate([q[0] for q in qs], axis=1), np.concatenate([q[1] for q in qs], axis=1))
def put(q, e, v):
    c, s = q[0].reshape(128, -1, 4).copy(), q[1].copy(); c[:, e] = v[0].reshape(128, -1, 4); s[:, e] = v[1]
    return (c.reshape(128, -1), s)
def pk(c, s):
    return (np.ascontiguousarray(c), mx_ref.live(s))
def emit(q):
    return q[0], q[1]
def packed(v, rng):
    q = [mx_ref.quantize(np.ascontiguousarray(v[r])) for r in range(N)]
    return np.stack([a for a, b in q]), np.stack([mx_ref.plane(b, rng) for a, b in q])
def values_of_codes():
    e, c = np.zeros((128, 128, 4), np.float32), np.zeros((128, 2, 4), np.uint8)
    e[np.arange(128), np.arange(128), 0] = 1
    c[:127, :, 0] = np.arange(256).reshape(2, 128).T[:127]
    return mx_ref.matmul(mx_ref.quantize(e.reshape(128, 512).astype(BF)), (c.reshape(128, 8), np.full((16, 2), 127, np.uint8))).T.reshape(-1).astype(np.float64)
CODE_VALUE, SCALE_VALUE = values_of_codes(), 2.0 ** (np.arange(256) - 127.0)
def decode(q):
    return (CODE_VALUE[q[0]].reshape(16, 8, -1, 4) * SCALE_VALUE[q[1]][:, None, :, None] + 0.0).reshape(128, -1).astype(np.float32)
def f(rng, *shape):
    return mx_ref.flush((rng.standard_normal(shape, dtype=np.float32) * np.exp2(rng.integers(-2, 3, shape[:-1] + (1,)))).astype(BF))
def wide(rng, *shape, cols=0):
    v = rng.standard_normal(shape, dtype=np.float32) * np.exp2(rng.integers(-12, 13, shape)).astype(np.float32)
    if cols: v *= np.repeat(np.exp2(rng.integers(-cols, cols + 1, shape[:-2] + (1, shape[-1] // 4))) * (rng.random(shape[:-2] + (1, shape[-1] // 4)) > 0.0625), 4, axis=-1).astype(np.float32)
    return mx_ref.flush(v.astype(BF))
C, S, R, SWEEPS = 192, 96, 3, 8
def big(v):
    v = v.astype(np.float32)
    v[np.abs(v) < np.float32(2.0 ** -16)] = 0
    return v
def numbers_of(rng):
    return big(f(rng, N, 128, 4 * C)).reshape(N, 8, 16, C, 4), f(rng, N, 128, 512).astype(np.float32).reshape(N, 128, 128, 4), f(rng, N, 128, 512).astype(np.float32)
def ring(rng, e):
    s, i, n = rng.permutation(C), np.arange(C), np.zeros((3, C), np.int64)
    n[0, s] = s[i ^ 1]
    n[1, s] = s[(((i + 1) ^ 1) - 1) % C]
    n[2, s[e]] = s[e[i ^ 1]]
    return n[rng.permutation(3)], s
def beside(a, b):
    return (a - b) % C in (1, C - 1)
def chords(rng):
    e = rng.permutation(C)
    for i in range(0, C, 2):
        if beside(e[i], e[i + 1]):
            for j in range(0, C, 2):
                if j != i and not beside(e[i], e[j + 1]) and not beside(e[j], e[i + 1]):
                    e[i + 1], e[j + 1] = e[j + 1], e[i + 1]
                    break
    return e
def opposite():
    i = np.arange(S)
    return np.stack([i, i + S], axis=1).reshape(-1)
def crossed(rng):
    i = 2 * np.arange(S)
    return np.stack([i, (i + 2 * rng.integers(1, S - 1) + 1) % C], axis=1).reshape(-1)
def fours(rng):
    s, i, n = rng.permutation(C), np.arange(C), np.zeros((3, C), np.int64)
    for k in range(3): n[k, s] = s[i ^ (k + 1)]
    return n
def graphs(rng):
    return np.stack([np.stack([ring(rng, chords(rng))[0] for g in range(8)]) for r in range(N)])
def layers(rng, still=()):
    w = (big(f(rng, N, 128, 2048)) * np.float32(0.03125)).reshape(N, 128, 512, 4)
    w *= np.where(np.sum(np.abs(w), axis=(1, 3), keepdims=True) > 28.0, 0.5, 1.0)
    w = w.reshape(N, 8, 16, 4, 8, 16, 4)
    for i in still:
        w[:, :, i] = 0
        w[:, :, :, :, :, i] = 0
    return w
def drawn(rng, x, u, v, n, w):
    c, s = packed(np.ascontiguousarray(w).reshape(N, 128, 2048).astype(np.float32).astype(BF), rng)
    e = [np.stack([gtable(n[r, :, k]) for r in range(N)]) for k in range(3)]
    return {"x": x.reshape(N, 128, 4 * C).astype(np.float32).astype(BF), "u": u.reshape(N, 128, 512).astype(np.float32).astype(BF), "v": v.reshape(N, 128, 512).astype(np.float32).astype(BF), "n0": e[0], "n1": e[1], "n2": e[2], "wc": c, "ws": s}
def whole(x, u, s, i, k):
    for m in range(3):
        x[:, i + m] = ((s[:, :, None] >> (4 * m + np.arange(4))) & 1) * (2.0 ** (4 * m + np.arange(4)) * k)
        for h in range(0, 128, 16): u[h + i + m, h] = 1.0
def setup_inputs(rng):
    x, u, v = numbers_of(rng)
    return drawn(rng, x, u, v, graphs(rng), layers(rng))
def setup_inputs_ties(rng):
    x, u, v = numbers_of(rng)
    n, o = graphs(rng), rng.permutation(N)
    u[:, :, ::16] = 0
    for r in range(N):
        whole(x[r], u[r], rng.integers(0, 3, (8, C)), 0, 1.0)
        if o[r] == 0: u[r][:, ::16] = 0
        if o[r] == 1: u[r][:, ::16] *= -1
        if o[r] == 2: n[r] = np.stack([fours(rng) for g in range(8)])
    return drawn(rng, x, u, v, n, layers(rng, (0, 1, 2)))
def setup_inputs_near(rng):
    x, u, v = numbers_of(rng)
    o = rng.permutation(N) % 4
    x[:, :, 0] = 0
    x[:, :, 8:] = 0
    u[:, :, ::16] = 0
    for r in range(N):
        b, k = rng.integers(0, 2, (8, C)), rng.permutation(8)
        x[r, :, 0, :, 0] = [1.0, -1.0, 1.0, 0.0][o[r]]
        if o[r] < 3:
            whole(x[r], u[r], rng.integers(0, 256, (8, C)), 8, 2.0 ** -23)
            x[r, :, 11, :, 0] = 2.0 ** -10
        else:
            x[r, :, 12, :, 0] = 2.0 ** -28 * (1 - b)
            x[r, :, 13, :, 0] = 1.125 * 2.0 ** -28 * b
            for g in k[2:6]: x[r, g, 14, :, 0] = 2.0 ** -28
        for g in k[:4]: x[r, g, 0, rng.integers(C), 0] = rng.choice([-1.0, 1.0]) * 2.0 ** 26
        for h in range(0, 128, 16):
            u[r, h, h, 0] = 1.0
            u[r, h + 11, h, 0] = 1.0
            u[r, h + 12, h, 0] = 1.25
            u[r, h + 13, h, 0] = 1.125
            u[r, h + 14, h, 0] = -1.25
        if o[r] >= 2: u[r][:, ::16] *= 2.0 ** -30
    return drawn(rng, x, u, v, graphs(rng), layers(rng, (0, 8, 9, 10, 11, 12, 13, 14, 15)))
def setup_inputs_long(rng):
    x, u, v = numbers_of(rng)
    k = (N, 8, 8, C, 4)
    x[:, :, 8:] = rng.choice([-1.0, 1.0], k) * (1.0078125 + 0.015625 * rng.integers(0, 64, k)) * 2.0 ** -rng.integers(8, 15, k)
    x[:, :, 8, :, 0] = 1.96875
    u[:, :, ::16] = 0
    n, o, t = np.zeros((N, 8, 3, C), np.int64), (np.arange(N) + rng.integers(N)) % N // (N // 2), np.arange(C)
    for r in range(N):
        s = np.zeros((8, C), np.int64)
        for g in range(8):
            n[r, g], a = ring(rng, crossed(rng) if o[r] else opposite())
            s[g, a] = 512 * (1 - t % 2) + rng.permutation(C) if o[r] else C - 1 - t
        whole(x[r], u[r], s, 0, 1.0)
    return drawn(rng, x, u, v, n, layers(rng, (0, 1, 2)))
def setup_inputs_ends(rng):
    x, u, v = numbers_of(rng)
    o, k, h = rng.permutation(N) % 4, rng.permutation(N) % 2, rng.permutation(8)
    sg = rng.choice([-1.0, 1.0], (8, 16, 4))
    sg[h[:4]] = rng.choice([-1.0, 1.0])
    row, i = sg.reshape(128, 4), np.arange(128)
    n, w = graphs(rng), np.zeros((N, 128, 4, 128, 4), np.float32)
    for r in range(N):
        c = rng.permutation(C) % 2 == 0
        size, turn = 2.0 ** 30, np.ones((8, 16, 1, 1))
        if o[r] == 0:
            m, s = ring(rng, crossed(rng))
            n[r] = m
            a = 0.9 + 0.1 * rng.random((8, 16, C, 4))
            a[:, :, s[::2]] -= 0.15
            a *= 2.0 ** 26
        elif o[r] == 1:
            n[r] = np.stack([fours(rng) for g in range(8)])
            a = np.ones((8, 16, C, 4)) * np.where(c, 2.0 ** 26, 2.0 ** 25)[:, None]
            a[h[4:]] = np.where(c, 2.0 ** 25, 2.0 ** 26)[:, None]
            turn[h[4:]] = -1
        elif o[r] == 2: a, size = 2.0 ** -30, 2.0 ** -30
        else: a = np.where(c, 2.0 ** 26, 2.0 ** -30)[:, None]
        x[r] = a * sg[:, :, None]
        u[r] = size * row[:, None] * (turn * np.ones((1, 16, 1, 1))).reshape(128, 1, 1) * rng.choice([-1.0, 1.0], (1, 128, 1))
        v[r] = (size * row[:, None] * rng.choice([-1.0, 1.0], (1, 128, 1))).reshape(128, 512)
        if k[r]:
            for b in range(4): w[r, i, b, i, b] = 32
        else: w[r] = 0.0625 * row[:, None, None] * row.T[None, :, :, None]
    return drawn(rng, x, u, v, n, w)
def setup_inputs_spread(rng):
    x, u, v = numbers_of(rng)
    return drawn(rng, big(wide(rng, N, 128, 4 * C, cols=6)), u, v, graphs(rng), layers(rng))
def check_inputs(d):
    b = []
    for k, t in (("x", 26), ("u", 30), ("v", 30)):
        a = np.abs(d[k].astype(np.float32))
        if not (np.isfinite(a).all() and ((a == 0) | (a >= 2.0 ** -30) & (a <= 2.0 ** t)).all()): b.append("a value of " + k)
    none, least, most = [emit(mx_ref.quantize(np.full((128, 16), k, np.float32).astype(BF)))[1][0, 0] for k in (0.0, 2.0 ** -30, 2.0 ** 30)]
    i = np.arange(C)
    for r in range(N):
        n = [gentries(d[k][r]) for k in ("n0", "n1", "n2")]
        if not all([((e >= 0) & (e < C)).all() for e in n]): b.append("an entry of n0, n1 or n2")
        else:
            if any([(np.take_along_axis(e, e, axis=1) != i).any() or (e == i).any() for e in n]): b.append("n0, n1, n2: nodes not in pairs")
            if ((n[0] == n[1]) | (n[0] == n[2]) | (n[1] == n[2])).any(): b.append("n0, n1, n2: equal neighbours")
        if ((d["wc"][r] & 0x7F) == 0x7F).any(): b.append("wc: a code that is no number")
        s = mx_ref.live(d["ws"][r])
        if ((s != none) & ((s < least) | (s > most))).any(): b.append("ws: a scale out of range")
        if not (np.sum(np.abs(decode(pk(d["wc"][r], d["ws"][r]))).reshape(128, 512, 4), axis=(0, 2), dtype=np.float64) <= 32).all(): b.append("W: the sizes of a column")
    return b
def look(t, e):
    return np.where(e < 0, -1, np.take_along_axis(t, np.maximum(e, 0), axis=2))
def around(t, nb):
    return np.stack([np.take_along_axis(t, e, axis=2) for e in nb])
def best(t, nb):
    a = around(t, nb)
    return np.where(np.max(a, axis=0) < 0, -1, np.take_along_axis(nb, np.argmax(a, axis=0)[None], axis=0)[0])
def reference(x, u, v, n0, n1, n2, wc, ws):
    qu = [mx_ref.quantize(u[r]) for r in range(N)]
    lay = [pk(wc[r], ws[r]) for r in range(N)]
    now = [x[r] for r in range(N)]
    nb = np.stack([np.stack([gentries(n[r]) for r in range(N)]) for n in (n0, n1, n2)]).astype(np.int64)
    node = np.arange(C)
    for t in range(R):
        qx = [mx_ref.quantize(now[r]) for r in range(N)]
        full = [decode(qx[r]).astype(BF) for r in range(N)]
        score = np.stack([mx_ref.matmul(qu[r], qx[r])[::16] for r in range(N)]) + np.float32(0.0)
        z = C - 1 - np.argsort(np.argsort(-score, axis=2, kind="stable"), axis=2)
        state = np.zeros((N, 8, C), np.int64)
        for i in range(SWEEPS):
            key = np.where(state == 0, 512 * np.count_nonzero(around(state, nb) == 2, axis=0) + z, -1)
            win = key > np.max(around(key, nb), axis=0)
            state[win] = 1
            state[(state == 0) & np.any(around(win, nb), axis=0)] = 2
        coarse = state == 1
        o = np.argsort(~coarse, axis=2, kind="stable")
        slot, head = np.argsort(o, axis=2), o[:, :, :S]
        c = np.where(np.take_along_axis(coarse, head, axis=2), head, -1)
        fine = best(np.where(coarse, -1, z), nb)
        p1 = np.where(coarse, node, best(np.where(coarse, z, -1), nb))
        p2 = np.where(coarse, node, np.where(fine < 0, p1, look(p1, fine)))
        cf, s1, s2 = look(fine, c), look(slot, p1), look(slot, p2)
        qe = []
        for r in range(N):
            e = (gcols(full[r], c[r]).astype(np.float32) + gcols(full[r], cf[r]).astype(np.float32)) * np.float32(0.5)
            qe.append(mx_ref.quantize(e.astype(BF)))
        for r in range(N):
            h = tile([mx_ref.matmul(pick(lay[r], np.arange(128 * b, 128 * b + 128)), qe[r - 1]) * np.float32(0.03125) for b in range(4)])
            add = ((gcols(h, s1[r]).astype(np.float32) + gcols(h, s2[r]).astype(np.float32)) * np.float32(0.5)).astype(BF)
            now[r] = (full[r].astype(np.float32) + add.astype(np.float32)).astype(BF)
    y, op = np.zeros((N, 128, C), np.float32), np.zeros((N, 8, C), np.float32)
    oc, osc = np.zeros((N, 128, 4 * C), np.uint8), np.zeros((N, 16, C), np.uint8)
    for r in range(N):
        q = mx_ref.quantize(now[r])
        y[r] = mx_ref.matmul(mx_ref.quantize(v[r]), q)
        op[r] = p1[r]
        oc[r], osc[r] = emit(q)
    return {"y": y, "op": op, "oc": oc, "osc": osc}

from concourse.mybir import dt, AluOpType, ActivationFunctionType

C, SL, ROUNDS, SWEEPS = 192, 96, 3, 8
BF, F32, F16, I32, U16, MXC, U8 = "bfloat16", "float32", "float16", "int32", "uint16", "float8_e4m3fn_x4", "uint8"
K = 256
BIG = 1024
E3 = 3 * C


def _sb(n, d):
    return ("sbuf", [128, n], d)


SCRATCH = {
    "xin": _sb(768, BF), "xs": _sb(768, BF), "uin": _sb(512, BF), "vin": _sb(512, BF),
    "qx": _sb(192, MXC), "sx": _sb(192, U8), "qu0": _sb(128, MXC), "su0": _sb(128, U8),
    "qu": _sb(128, MXC), "su": _sb(128, U8), "qv": _sb(128, MXC), "sv": _sb(128, U8),
    "qw": _sb(512, MXC), "sw": _sb(512, U8), "eb": _sb(2048, BF), "qb": _sb(512, MXC), "sbb": _sb(512, U8),
    "et": _sb(512, BF),
    "nt": _sb(36, I32), "n16": _sb(36, U16), "iota": _sb(200, F32), "pc": _sb(2, I32), "pf": _sb(1, F32),
    "ic": _sb(2, I32), "icf": _sb(2, F32), "vw": _sb(36, F32), "uoff": _sb(8, U16),
    "da": _sb(16, BF), "db": _sb(16, BF), "dx": _sb(576, BF), "dx8": _sb(192, BF),
    "cb": _sb(1, F32), "ca": _sb(1, F32), "c8": _sb(1, F32), "tiny": _sb(1, F32),
    "npp": _sb(12, F32), "nff": _sb(12, F32), "ntp": _sb(12, F32), "kb": _sb(3, F32),
    "lt": _sb(72, F32), "lt2": _sb(72, F32), "lt3": _sb(72, F32), "lcmp": _sb(72, U16),
    "r3": _sb(576, BF), "x3": _sb(576, F16), "la": _sb(36, U16),
    "rc": _sb(576, BF), "ra": _sb(576, BF), "dw": _sb(576, BF), "zero": _sb(576, BF), "rcnt": _sb(432, BF),
    "o5d": _sb(960, BF), "o5": _sb(960, F16), "o5o": _sb(960, F16), "dp": _sb(576, F16), "df": _sb(576, F16),
    "sa": _sb(192, BF), "sb2": _sb(192, BF), "sc2": _sb(192, F16),
    "w": _sb(384, F32), "ab": _sb(192, F32), "g0": _sb(192, F32), "g1": _sb(192, F32),
    "b3": _sb(576, BF), "yy": _sb(192, BF),
    "ga": _sb(576, BF), "oa": _sb(576, BF), "ob": _sb(576, BF), "ocs": _sb(576, BF),
    "cf": _sb(576, BF), "inc": _sb(208, BF), "cnt": _sb(432, BF), "cno": _sb(432, BF), "junk": _sb(576, BF),
    "acc": _sb(3, F32), "lh": _sb(6, U16),
    "fb": _sb(768, BF), "ef": _sb(800, F32), "hh": _sb(448, BF), "gs": _sb(768, BF), "tb": _sb(768, BF),
    "tps": _sb(576, F16), "pps": _sb(576, F16), "fps": _sb(576, F16),
    "xt": _sb(192, F32), "xp": _sb(192, F32), "xf": _sb(192, F32), "xc": _sb(192, F16), "x1": _sb(192, F16),
    "ti": _sb(12, I32), "tj": _sb(12, I32), "ltop": _sb(12, U16),
    "cw": _sb(12, F32), "zf": _sb(12, F32), "zp": _sb(12, F32), "a1": _sb(12, F32), "a2": _sb(12, F32),
    "pi": _sb(12, I32), "fi": _sb(12, I32), "pj": _sb(12, I32), "fj": _sb(12, I32),
    "lp": _sb(12, U16), "lf": _sb(12, U16), "s1r": _sb(192, BF), "l1": _sb(12, U16),
    "s2r": _sb(192, BF), "x2": _sb(192, F16), "l2": _sb(12, U16), "so": _sb(192, F32), "fc": _sb(768, BF),
    "opr": _sb(192, F32), "ys": _sb(192, F32),
    "psd": ("psum", [128, 2048], F32), "psr": ("psum", [128, 2048], F32),
}
for _t in range(ROUNDS):
    SCRATCH["qe%d" % _t] = _sb(128, MXC)
    SCRATCH["se%d" % _t] = _sb(128, U8)
    SCRATCH["ql%d" % _t] = _sb(224, MXC)
    SCRATCH["sl%d" % _t] = _sb(224, U8)

POOL = {"V": 56, "S": 30, "P": 14, "G": 22}
NDMA = 20
SEMAPHORES = (["%s%d" % (q.lower(), i) for q in POOL for i in range(POOL[q])] + ["d%d" % i for i in range(NDMA)]
              + ["arr%d" % t for t in range(ROUNDS)] + ["sent"])

A = AluOpType
AF = ActivationFunctionType


def v(name, a=0, b=None, s=1):
    if b is None:
        b = SCRATCH[name][1][1]
    return ("v", name, a, b, s)


def place(name, k):
    return v(name, k, E3, 3)


def ind(win, off):
    return ("i", win, off)


def _mask(x):
    name, a, b, s = x[1:]
    if SCRATCH[name][0] == "psum":
        return 1 << (a // 512)
    if s == 1:
        return ((1 << b) - 1) ^ ((1 << a) - 1)
    m = 0
    for i in range(a, b, s):
        m |= 1 << i
    return m


def plan(pre_ns, e1, e2):
    key = (pre_ns, e1, e2)
    if key in _PLANS:
        return _PLANS[key]
    best = None
    for x in range(0, 321, 32):
        for y in range(x, E3, 32):
            for z in range(y + 32, E3 + 1, 32):
                for join in range(4):
                    if (join & 1 and not (x and y > x)) or (join & 2 and not y):
                        continue
                    total = 0.0
                    for wake, el, f in ((40.0, 1.1, 1.0), (80.0, 1.4, 1.15), (150.0, 1.9, 1.3), (60.0, 1.9, 1.15)):
                        t1 = wake + (65 + el * x if x else 0)
                        t2 = t1 + 65 + el * (z - y)
                        t3 = t2 + (65 + el * (E3 - z) if z < E3 else 0)
                        tp = max(wake, e1 * f / 1.15) + pre_ns * f / 1.15
                        tg = tp + (50 + el * (y - x) if y > x else 0)
                        tv = tg + e2 * f / 1.15
                        cuts = []
                        if x and not join & 1:
                            cuts.append((x, t1))
                        if y > x and not join & 2:
                            cuts.append((y, max(t1, tg)))
                        cuts.append((z, max(t2, tg)))
                        if z < E3:
                            cuts.append((E3, t3))
                        a = 0
                        for c, ready in cuts:
                            c = 3 * (c // 3)
                            tv = max(tv, ready + wake, tp + wake) + f * max(53.0, 0.415 * (c - a))
                            a = c
                        total += tv / el
                    if best is None or total < best[0]:
                        best = (total, x, y, z, [3 * (c // 3) for c, ready in cuts])
    _PLANS[key] = best[1:]
    return best[1:]


_PLANS = {}


def rank_program(g, core, T, topo):
    rank = T.rank_of(core)
    if rank is None:
        return
    n = len(T.cores)
    nxt = T.cores[(rank + 1) % n]
    rid, pid = topo.addr(nxt, core)
    eng = topo.engines(core, nxt)
    eng = eng[::max(1, len(eng) // 8)]
    emask = sum(1 << e for e in eng)
    Q = {"V": g.vector, "S": g.scalar, "P": g.tensor, "G": g, "Y": g.sync}
    ops = []

    def ap(x):
        if not isinstance(x, tuple):
            return x
        if x[0] == "i":
            return ap(x[1]).indirect(ap(x[2]))
        if x[4] == 1:
            return T[x[1]][:, x[2]:x[3]]
        return T[x[1]][:, x[2]:x[3]:x[4]]

    def views(xs):
        out = []
        for x in xs:
            if isinstance(x, tuple):
                if x[0] == "i":
                    out += [x[1], x[2]]
                else:
                    out.append(x)
        return [(x[1], _mask(x)) for x in out]

    def rec(q, fn, w, r, kind="c"):
        ops.append({"q": q, "fn": fn, "w": views(w), "r": views(r), "kind": kind})

    def cp(o, i):
        rec("V", lambda: g.vector.tensor_copy(ap(o), ap(i)), [o], [i])

    def tt(o, a, b, op):
        rec("V", lambda: g.vector.tensor_tensor(ap(o), ap(a), ap(b), op), [o], [a, b])

    def ts(o, a, s1, op0, s2=None, op1=None):
        if op1 is None:
            rec("V", lambda: g.vector.tensor_scalar(ap(o), ap(a), ap(s1), None, op0), [o], [a, s1])
        else:
            rec("V", lambda: g.vector.tensor_scalar(ap(o), ap(a), ap(s1), ap(s2), op0, op1), [o], [a, s1, s2])

    def scan(o, d0, d1, init, op0, op1):
        rec("V", lambda: g.vector.tensor_tensor_scan(ap(o), ap(d0), ap(d1), init, op0, op1), [o], [d0, d1])

    def ms(o, c):
        rec("V", lambda: g.vector.memset(ap(o), c), [o], [])

    def quant(q, s, i):
        rec("V", lambda: g.vector.quantize_mx(ap(q), ap(s), ap(i)), [q, s], [i])

    def act(o, i, f, bias=None, scale=None, acc=None):
        kw = {}
        if bias is not None:
            kw["bias"] = bias
        if scale is not None:
            kw["scale"] = scale
        if acc is not None:
            kw["accum_out"] = acc
        rec("S", lambda: g.scalar.activation(ap(o), ap(i), f, **{k: ap(x) for k, x in kw.items()}),
            [o, acc], [i, bias])

    def mm(o, l, ls, r, rs):
        rec("P", lambda: g.tensor.matmul_mx(ap(o), ap(l), ap(ls), ap(r), ap(rs), True, True), [o], [l, ls, r, rs])

    def iota(o, pat, base, cm):
        if SCRATCH[o[1]][2] == I32:
            rec("G", lambda: g.iota(ap(o), pat, base, cm), [o], [])
        else:
            rec("G", lambda: g.iota(ap(o), pat, base, cm, allow_small_or_imprecise_dtypes=True), [o], [])

    def dma(q, o, i, w, r):
        rec(q, lambda: Q[q].dma_start(o(), i()), w, r, "dma")

    def load(q, dst, src, cast=False):
        if cast:
            dma(q, lambda: ap(dst).bitcast(dt.uint8), lambda: src[:], [dst], [])
        else:
            dma(q, lambda: ap(dst), lambda: src[:], [dst], [])

    def extract(o, row, table):
        scan(o, table, row, 0.0, A.add, A.max)

    def kept(name, width):
        return v(name, 15, width, 16)

    def bank(name, b, m):
        return v(name, 512 * b, 512 * b + m)

    load("Y", v("nt", 0, 12), T.n0)
    load("S", v("uin"), T.u)
    load("Y", v("xin"), T.x)
    load("S", v("nt", 12, 24), T.n1)
    load("Y", v("nt", 24, 36), T.n2)
    load("Y", v("qw"), T.wc, True)
    load("Y", v("sw"), T.ws)
    load("Y", v("vin"), T.v)
    iota(v("pc"), [[1, 2]], 0, 1)
    iota(v("iota", 0, C), [[1, C]], 0, 0)
    iota(v("pf"), [[1, 1]], 0, 1)
    iota(v("rc"), [[0, C], [-2, 3]], 1, 0)
    iota(place("ra", 1), [[0, C]], 64, 0)
    iota(v("zero"), [[0, E3]], 0, 0)
    iota(v("et"), [[0, 512]], 0, 0)
    for k, c in enumerate((0, 1, -1, 1, 1)):
        iota(v("o5d", k, 960, 5), [[0, C]], c, 0)
    iota(v("ef"), [[0, 800]], 0, 0)
    iota(v("cf"), [[0, E3]], 0, 0)
    iota(v("inc"), [[0, 208]], 0, 0)
    iota(v("rcnt"), [[0, 3], [200, 144]], 0, 0)
    iota(v("hh"), [[0, 448]], 0, 0)
    iota(v("iota", C, 200), [[0, 8]], -1, 0)

    ms(v("eb"), 0.0)
    ts(v("ic"), v("pc"), 15, A.bitwise_and)
    cp(v("uoff"), v("iota", 0, 128, 16))
    ms(v("tiny"), 2.0 ** -122)
    cp(v("icf"), v("ic"))
    for b in range(4):
        ts(v("eb", 512 * b + b, 512 * b + 512, 4), v("iota", 0, 128), v("pf"), A.is_equal)
    for k in range(3):
        ts(v("vw", 12 * k, 12 * k + 12), v("iota", 0, C, 16), v("icf", 0, 1), A.add)
    ts(v("da"), v("iota", 0, 16), v("icf", 0, 1), A.is_equal, -2.0 * BIG, A.mult)
    ts(v("db"), v("iota", 0, 16), v("icf", 1, 2), A.is_equal, float(BIG), A.mult)
    ts(v("cb"), v("icf", 0, 1), 15.0, A.is_lt, float(BIG), A.mult)
    quant(v("qu0"), v("su0"), v("uin"))
    quant(v("qx"), v("sx"), v("xin"))
    rec("V", lambda: g.vector.tensor_copy(T.qu[:, 0:128].bitcast(dt.uint32),
                                          T.qu0[:, 0:128].bitcast(dt.uint32).indirect(T.uoff[:, 0:8])),
        [v("qu")], [v("qu0"), v("uoff")])
    act(v("su"), ind(v("su0"), v("uoff")), AF.Copy)
    wd = [16]

    def double():
        m = min(wd[0], E3 - wd[0])
        cp(v("dx", wd[0], wd[0] + m), v("dx", 0, m))
        wd[0] += m

    def row(k):
        act(place("r3", k), ind(v("iota", 0, C), v("n16", 12 * k, 12 * k + 12)), AF.Copy)

    cp(v("n16"), v("nt"))
    tt(v("lt", 0, 36), v("nt"), v("vw"), A.is_gt)
    row(0)
    tt(v("dx", 0, 16), v("da"), v("db"), A.add)
    ts(v("lt2", 0, 36), v("lt", 0, 36), float(C), A.mult)
    double()
    tt(v("lt3", 0, 36), v("lt2", 0, 36), v("nt"), A.add)
    double()
    cp(v("lcmp", 0, 36), v("lt3", 0, 36))
    double()

    def hop(win, vget, sget, fin, pre, extra):
        first, second = extra
        x, y, z, cuts = plan(95 if pre else 0, sum(e[0] for e in first), sum(e[0] for e in second))
        for a, b in ((0, x), (y, z), (z, E3)):
            if b > a:
                sget(v("ga", a, b), ind(win, v("la", a // 16, b // 16)))
        for e in first:
            e[1]()
        if pre:
            pre()
        if y > x:
            vget(v("ga", x, y), ind(win, v("la", x // 16, y // 16)))
        for e in second:
            e[1]()
        a = 0
        for c in cuts:
            fin(a, c)
            a = c

    def hop_c(first, extra):
        fin = lambda a, b: scan(v("ocs", a, b), v("rc", a, b), v("ga", a, b), 1.0, A.max, A.min)
        if first:
            hop(v("oa"), lambda o, i: ts(o, i, -2.0, A.mult, 1.0, A.add),
                lambda o, i: act(o, i, AF.Identity, 1.0, -2.0), fin, None, extra)
        else:
            hop(v("ob"), lambda o, i: ts(o, i, -1.0, A.max, 1.0, A.min),
                lambda o, i: act(o, i, AF.Sign), fin, None, extra)

    def hop_a(extra):
        hop(v("ocs"), lambda o, i: ts(o, i, -2.0, A.mult, 18.0, A.add),
            lambda o, i: act(o, i, AF.Identity, 18.0, -2.0),
            lambda a, b: scan(v("oa", a, b), v("ra", a, b), v("ga", a, b), 64.0, A.min, A.add),
            lambda: ts(place("ra", 2), place("ocs", 2), 20.0, A.mult, 40.0, A.add), extra)

    def hop_b(extra):
        hop(v("oa"), cp, lambda o, i: act(o, i, AF.Copy),
            lambda a, b: scan(v("ob", a, b), v("ga", a, b), v("dw", a, b), -64.0, A.max, A.add),
            lambda: ts(place("dw", 2), place("oa", 2), -1.0, A.mult), extra)

    def cmp(o, j, other):
        tt(o, ind(v("w"), v("lcmp", 12 * j, 12 * j + 12)), other, A.is_lt)

    def unpack():
        for b in range(4):
            mm(bank("psd", b, C), v("qb", 128 * b, 128 * b + 128), v("sbb", 128 * b, 128 * b + 128), v("qx"), v("sx"))

    def nbr(k):
        act(v("g%d" % k), ind(v("w", 0, C), v("n16", 12 * k, 12 * k + 12)), AF.Copy)

    def plane(b):
        act(v("fb" if b < 4 else "fc", C * (b % 4), C * (b % 4) + C), bank("psd", b % 4, C), AF.Copy)

    def pot(name, k, f):
        return (95, lambda: ts(place(name, k), v("o5o", 3 * k - 2, 960, 5), f * K, A.mult))

    def e_full(b):
        fbb = v("fb", C * b, C * b + C)
        return (320, lambda: tt(v("ef", 200 * b, 200 * b + C), ind(fbb, v("ltop")), v("fc", C * b, C * b + C), A.add))

    def consts():
        quant(v("qb"), v("sbb"), v("eb"))
        unpack()

    for t in range(ROUNDS):
        mm(bank("psr", 0, C), v("qu"), v("su"), v("qx"), v("sx"))
        mm(bank("psr", 1, C), v("qu"), v("su"), v("qx"), v("sx"))
        if t:
            unpack()
        act(v("ab"), bank("psr", 0, C), AF.Abs, v("tiny"), 0.625 * 2.0 ** -23)
        cp(v("w", 0, C), bank("psr", 1, C))
        if t == 0:
            double()
        tt(v("w", C, 2 * C), bank("psr", 1, C), v("ab"), A.subtract)
        act(v("so"), bank("psr", 0, C), AF.Copy)
        if t == 0:
            row(1)
            row(2)
            double()
        nbr(0)
        nbr(1)
        for k in range(3):
            cmp(place("b3", k), k, v("so"))
            if t == 0 and k == 0:
                double()
                ts(v("ca"), v("cb"), 3.0, A.mult, -2.0, A.add)
        if t == 0:
            extract(v("x3"), v("r3"), v("dx"))
        else:
            plane(0)
        scan(v("oa"), v("rc"), v("b3"), 1.0, A.max, A.min)
        if t == 0:
            ts(v("la"), kept("x3", E3), 3.0, A.mult, v("ca"), A.subtract)

        ex = [([], []) for _ in range(3 * (SWEEPS - 1))]
        ex[0][0].append((95, lambda: ts(place("dw", 1), place("b3", 1), -4.0, A.mult, 2.0, A.add)))
        ex[0][1].append((95, lambda: ts(v("yy"), place("b3", 0), -4.0, A.mult, 2.0, A.add)))
        ex[1][0].append((185, lambda: tt(v("dw", 0, 288, 3), v("yy", 0, 96), v("dw", 1, 288, 3), A.subtract)))
        ex[2][0].append((185, lambda: tt(v("dw", 288, E3, 3), v("yy", 96, C), v("dw", 289, E3, 3), A.subtract)))
        later = []
        if t == 0:
            later += [(540, consts),
                      (62, lambda: tt(v("lt", 36, 60), v("nt", 12, 36), v("nt", 0, 24), A.is_gt)),
                      (62, lambda: tt(v("lt", 60, 72), v("nt", 24, 36), v("nt", 0, 12), A.is_gt)),
                      (62, lambda: ts(v("lt2", 36, 72), v("lt", 36, 72), float(C), A.mult)),
                      (62, lambda: tt(v("lt3", 36, 60), v("lt2", 36, 60), v("nt", 12, 36), A.add)),
                      (62, lambda: tt(v("lt3", 60, 72), v("lt2", 60, 72), v("nt", 24, 36), A.add)),
                      (62, lambda: cp(v("lcmp", 36, 72), v("lt3", 36, 72))),
                      (370, lambda: tt(v("sa"), place("r3", 0), place("r3", 1), A.subtract)),
                      (370, lambda: tt(v("sb2"), place("r3", 1), place("r3", 2), A.subtract)),
                      (95, lambda: ts(v("o5", 0, 960, 5), v("sa"), -2.0 * K, A.add, 0.25 / K, A.mult)),
                      (95, lambda: ts(v("sc2"), v("sb2"), -1.0 * K, A.add, 0.5 / K, A.mult)),
                      (95, lambda: ts(v("dx8"), v("dx", 0, C), 8.0, A.mult)),
                      (370, lambda: tt(v("o5", 2, 960, 5), v("sc2"), v("o5", 0, 960, 5), A.add)),
                      (62, lambda: ts(v("c8"), v("cb"), 8.0, A.mult)),
                      (95, lambda: ts(place("dp", 0), v("zero", 0, C), -8192.0, A.add)),
                      (95, lambda: ts(place("df", 0), v("zero", 0, C), 8192.0, A.add)),
                      (62, lambda: ts(v("npp"), v("nt", 24, 36), v("c8"), A.subtract)),
                      (62, lambda: ts(v("nff"), v("nt", 24, 36), v("c8"), A.add)),
                      (62, lambda: ts(v("ntp"), v("nt", 24, 36), v("c8"), A.subtract, 2048.0, A.add)),
                      (62, lambda: ts(v("kb"), v("vw", 0, 3), -1.0, A.mult, -0.5, A.add))]
            later += [(150, lambda r=r: quant(v("ql%d" % r, SL, 224), v("sl%d" % r, SL, 224), v("et"))) for r in range(ROUNDS)]
        if t == 1:
            later.append((150, lambda: quant(v("qv"), v("sv"), v("vin"))))
        later += [(320, lambda: cmp(v("o5", 1, 960, 5), 3, v("g0"))),
                  (320, lambda: cmp(v("o5", 4, 960, 5), 4, v("g1"))),
                  (320, lambda: cmp(v("o5", 3, 960, 5), 5, v("g0")))]
        np5, np3 = (1, 1) if t == 0 else (4, 2)
        for a in range(0, 960, 960 // np5):
            later.append((460 // np5, lambda a=a, b=a + 960 // np5:
                          scan(v("o5o", a, b), v("o5d", a, b), v("o5", a, b), 0.0, A.mult, A.add)))
        later += [pot("dp", 1, 4.0), pot("dp", 2, 2.0)]
        for a in range(0, E3, E3 // np3):
            later.append((280 // np3, lambda a=a, b=a + E3 // np3:
                          scan(v("tps", a, b), v("dp", a, b), v("zero", a, b), 0.0, A.add, A.max)))
        for a in range(0, C, C // np3):
            later.append((190 // np3, lambda a=a, b=a + C // np3:
                          extract(v("xt", a, b), v("tps", 3 * a + 2, 3 * b, 3), v("dx8", a, b))))
        later += [(62, lambda: tt(v("ti"), kept("xt", C), v("ntp"), A.add)),
                  (62, lambda: ts(v("tj"), v("ti"), K - 1, A.bitwise_and)),
                  (62, lambda: cp(v("ltop"), v("tj"))),
                  pot("df", 1, -4.0), pot("df", 2, -2.0)] + [e_full(b) for b in range(4)]
        gaps = [ex[h][k] for h in range(3, len(ex)) for k in range(2) if h % 3 == 0 or k == 0]
        for i in range(len(later)):
            gaps[i * len(gaps) // len(later)].append(later[i])
        side = [lambda: act(place("ra", 0), place("b3", 2), AF.Copy)]
        side += [None, None, None, None, lambda: plane(0), lambda: plane(1)] if t == 0 else [lambda: plane(1)]
        side += [lambda b=b: plane(b) for b in range(2, 8)]
        for h in range(len(ex)):
            if h % 3 == 0:
                hop_c(h == 0, ex[h])
            elif h % 3 == 1:
                hop_a(ex[h])
            else:
                hop_b(ex[h])
            if h < len(side) and side[h]:
                side[h]()

        ts(place("cf", 2), place("ob", 2), 0.0, A.is_lt)
        scan(v("inc", 0, C), v("zero", 0, C), place("cf", 2), 0.0, A.add, A.add)
        for c in range(3):
            act(v("junk", C * c, C * c + C), v("inc", 0, C), AF.Sign, v("kb", c, c + 1), None, v("acc", c, c + 1))
        for c in range(3, 6):
            ts(v("cnt", 144 * (c - 3), 144 * (c - 2)), v("inc", 48, C), v("vw", c, c + 1), A.is_le)
        extract(v("xc"), place("cf", 2), v("dx", 0, C))
        scan(v("cno"), v("rcnt"), v("cnt"), 0.0, A.min, A.add)
        ts(v("lh", 0, 3), v("acc"), -0.5, A.mult, C / 2.0, A.add)
        ts(v("lh", 3, 6), v("cno", 143, 432, 144), 48.0, A.add)
        for b in range(4):
            o, i = v("et", b, 4 * SL, 4), ind(v("ef", 200 * b, 200 * b + 200), v("lh"))
            if b < 2:
                act(o, i, AF.Copy, None, 0.5)
            else:
                ts(o, i, 0.5, A.mult)
        qe, se, ql, sl = "qe%d" % t, "se%d" % t, "ql%d" % t, "sl%d" % t
        ts(v("cw"), kept("xc", C), v("cb"), A.subtract, 8.0 * K, A.mult)
        quant(v(qe), v(se), v("et"))

        def send(src, dst, cast, t=t):
            if cast:
                f = lambda: g.remote_dma(T[dst][:, 0:SL].bitcast(dt.uint8), T[src][:, 0:SL].bitcast(dt.uint8),
                                         T.sem["arr%d" % t], T.sem.sent, pid, rid, emask)
            else:
                f = lambda: g.remote_dma(T[dst][:, 0:SL], T[src][:, 0:SL], T.sem["arr%d" % t], T.sem.sent, pid, rid, emask)
            rec("G", f, [], [v(src, 0, SL)], "send")

        send(qe, ql, True)
        send(se, sl, False)

        gx = 192
        act(v("ga", gx, E3), ind(v("cf"), v("la", gx // 16, 36)), AF.Identity, -4.0 * K, 8.0 * K)
        ts(v("ga", 0, gx), ind(v("cf"), v("la", 0, gx // 16)), 8.0 * K, A.mult, -4.0 * K, A.add)
        tt(v("zf"), v("cw"), v("vw", 0, 12), A.add)
        scan(v("pps"), v("dp"), v("ga"), 0.0, A.add, A.max)
        ts(v("zp"), v("zf"), float(C), A.max)
        extract(v("xp"), place("pps", 2), v("dx8"))
        scan(v("fps"), v("df"), v("ga"), 0.0, A.add, A.min)
        tt(v("a1"), kept("xp", C), v("npp"), A.add)
        extract(v("xf"), place("fps", 2), v("dx8"))
        tt(v("pi"), v("a1"), v("zp"), A.max)
        tt(v("a2"), v("nff"), kept("xf", C), A.subtract)
        ts(v("pj"), v("pi"), K - 1, A.bitwise_and)
        tt(v("fi"), v("a2"), v("zf"), A.max)
        cp(v("lp"), v("pj"))
        ts(v("fj"), v("fi"), K - 1, A.bitwise_and)
        act(v("s1r", 96, C), ind(v("inc"), v("lp", 6, 12)), AF.Copy)
        cp(v("s1r", 0, 96), ind(v("inc"), v("lp", 0, 6)))
        cp(v("lf"), v("fj"))
        extract(v("x1"), v("s1r"), v("dx", 0, C))
        act(v("s2r", 96, C), ind(v("s1r"), v("lf", 6, 12)), AF.Copy)
        cp(v("s2r", 0, 96), ind(v("s1r"), v("lf", 0, 6)))
        ts(v("l1"), kept("x1", C), v("cb"), A.subtract)
        extract(v("x2"), v("s2r"), v("dx", 0, C))
        ts(v("l2"), kept("x2", C), v("cb"), A.subtract)
        if t == ROUNDS - 1:
            cp(v("opr"), ind(v("iota"), v("lp")))
            dma("Y", lambda: T.op[:], lambda: T.opr[0:128:16, :], [], [v("opr")])

        rec(None, ("arr%d" % t, 2 * len(eng)), [v(ql, 0, SL), v(sl, 0, SL)], [], "arr")
        for b in range(4):
            mm(bank("psr", b, 128), v("qw", 128 * b, 128 * b + 128), v("sw", 128 * b, 128 * b + 128),
               v(ql, 0, 128), v(sl, 0, 128))

        def half(b):
            act(v("hh", 112 * b + 1, 112 * b + 1 + SL), bank("psr", b, SL), AF.Copy, None, 2.0 ** -6)

        half(0)
        cp(v("gs", 0, 128), ind(v("hh", 0, 112), v("l1", 0, 8)))
        for b in range(4):
            if b < 3:
                half(b + 1)
            a = 128 if b == 0 else 0
            act(v("gs", C * b + a, C * b + C), ind(v("hh", 112 * b, 112 * b + 112), v("l1", a // 16, 12)), AF.Copy)
        for b in range(5):
            if b < 4:
                tt(v("tb", C * b, C * b + C), ind(v("hh", 112 * b, 112 * b + 112), v("l2")),
                   v("gs", C * b, C * b + C), A.add)
            if b:
                tt(v("xs", b - 1, 768, 4), bank("psd", b - 1, C), v("tb", C * (b - 1), C * b), A.add)
        quant(v("qx"), v("sx"), v("xs"))

    mm(bank("psr", 0, C), v("qv"), v("sv"), v("qx"), v("sx"))
    dma("Y", lambda: T.oc[:], lambda: T.qx[:, 0:C].bitcast(dt.uint8), [], [v("qx")])
    cp(v("ys"), bank("psr", 0, C))
    for k in range(4):
        dma("S" if k < 2 else "Y", lambda k=k: T.osc[4 * k:4 * k + 4, :], lambda k=k: T.sx[32 * k:32 * k + 4, 0:C], [], [v("sx")])
    dma("S", lambda: T.y[:], lambda: T.ys[:], [], [v("ys")])

    hist = {}
    known = {q: 0 for q in Q}
    anc, waits, used = [], [], set()
    for i, o in enumerate(ops):
        deps = set()
        for name, m in o["w"]:
            for j, mj, wj in hist.get(name, []):
                if m & mj:
                    deps.add(j)
        for name, m in o["r"]:
            ps = SCRATCH[name][0] == "psum"
            for j, mj, wj in hist.get(name, []):
                if m & mj and (wj or (ps and ops[j]["q"] != o["q"])):
                    deps.add(j)
        mine = []
        if o["q"] is not None:
            for j in sorted(deps, reverse=True):
                if not known[o["q"]] >> j & 1:
                    mine.append(j)
                    used.add(j)
                    known[o["q"]] |= (1 << j) | anc[j]
            anc.append(known[o["q"]])
        else:
            anc.append(0)
        waits.append(mine)
        for name, m in o["w"]:
            hist.setdefault(name, []).append((i, m, True))
        for name, m in o["r"]:
            hist.setdefault(name, []).append((i, m, False))

    token, last, count, nd, tail = {}, {q: [] for q in POOL}, {}, [0], []
    for i, o in enumerate(ops):
        if o["kind"] == "arr":
            token[i] = o["fn"]
            continue
        for j in waits[i]:
            Q[o["q"]].wait_ge(T.sem[token[j][0]], token[j][1])
        ins = o["fn"]()
        if o["kind"] == "dma":
            name = "d%d" % nd[0]
            nd[0] += 1
            ins.then_inc(T.sem[name], 16)
            token[i] = (name, 16)
            if i not in used:
                tail.append(token[i])
        elif o["kind"] == "c" and i in used:
            pool = last[o["q"]]
            k = None
            for c in range(len(pool)):
                if anc[i] >> pool[c] & 1:
                    k = c
                    break
            if k is None:
                k = len(pool)
                pool.append(i)
            pool[k] = i
            name = "%s%d" % (o["q"].lower(), k)
            count[name] = count.get(name, 0) + 1
            ins.then_inc(T.sem[name], 1)
            token[i] = (name, count[name])
    g.wait_ge(T.sem.sent, 2 * ROUNDS * len(eng))
    for name, c in tail:
        g.wait_ge(T.sem[name], c)
